import numpy as np
import ml_dtypes


def mxq(x, axis, fmt="e4m3"):
    dtype, down = {"e4m3": (ml_dtypes.float8_e4m3fn, 7), "e5m2": (ml_dtypes.float8_e5m2, 14)}[fmt]
    v = np.moveaxis(np.asarray(x, np.float32).astype(ml_dtypes.bfloat16).astype(np.float64), axis, -1)
    blocks = v.reshape(v.shape[:-1] + (-1, 32))
    amax = np.abs(blocks).max(-1, keepdims=True)
    byte = np.maximum(np.where(amax > 0, np.frexp(amax)[1] - 1 + 127, 0) - down, 1)
    scale = np.exp2(byte - 127.0)
    codes = (blocks / scale).astype(np.float32).astype(dtype).astype(np.float64)
    return np.moveaxis((codes * scale).reshape(v.shape), -1, axis)


WIDE = False


def mx_kscale(k):
    if not WIDE:
        return np.ones(k)
    levels = np.array([30, -30])
    if k % 512:
        return np.exp2(np.random.permutation(np.resize(levels, k // 32))).repeat(32)
    a = np.empty((k // 512, 16))
    for p in range(k // 512):
        a[p, :8] = np.random.permutation(np.resize(levels, 8))
        for g in range(8):
            far = levels[np.abs(levels - a[p, g]) >= 10]
            a[p, g + 8] = far[np.random.randint(len(far))]
    return np.exp2(a.ravel()).repeat(32)


def f64(x):
    return np.asarray(x).astype(np.float64)


def striped(idx):
    return np.tile(np.asarray(idx).reshape(-1, 16).T, (8, 1)).astype(np.uint16)


def unstriped(offs):
    return offs[:16].T.reshape(-1).astype(np.int64)


def striped8(idx):
    return np.asarray(idx).reshape(8, -1, 16).transpose(0, 2, 1).reshape(128, -1).astype(np.uint16)


def unstriped8(offs):
    return offs.reshape(8, 16, -1).transpose(0, 2, 1).reshape(8, -1).astype(np.int64)


def pick8(x, idx, run):
    r = np.arange(len(x))
    return x[r[:, None], idx[r % (8 * run) // run]]


E2M1 = np.array([0.0, 0.5, 1.0, 1.5, 2.0, 3.0, 4.0, 6.0, -0.0, -0.5, -1.0, -1.5, -2.0, -3.0, -4.0, -6.0])


def pack_weight(w, fmt):
    k, n = w.shape
    w = f64(np.asarray(w, np.float32).astype(ml_dtypes.bfloat16)).reshape(k // 32, 32, n)
    amax = np.abs(w).max(1)
    if fmt in ("e4m3", "e5m2"):
        byte = np.frexp(amax)[1] - 1 + 127 - (7 if fmt == "e4m3" else 14)
    else:
        mant, ex = np.frexp(amax / 6.0)
        byte = np.where(mant > 0.5, ex, ex - 1) + 127
    byte = np.clip(np.where(amax > 0, byte, 1), 1, 254)
    scaled = (w * np.exp2(127.0 - byte)[:, None, :]).reshape(k, n).astype(np.float32)
    by_word = np.ascontiguousarray(scaled.reshape(k // 512, 128, 4, n).transpose(0, 1, 3, 2))
    if fmt in ("e4m3", "e5m2"):
        words = by_word.astype(ml_dtypes.float8_e4m3fn if fmt == "e4m3" else ml_dtypes.float8_e5m2).view(np.uint8)
    else:
        c = by_word.astype(ml_dtypes.float4_e2m1fn).view(np.uint8) & 0xF
        words = (c[..., 0::2] | (c[..., 1::2] << 4)).reshape(k // 512, 128, 2 * n)
    return np.ascontiguousarray(words), np.ascontiguousarray(byte.astype(np.uint8).reshape(k // 512, 16, n))


def unpack_weight(words, scales, fmt):
    g, _, n = scales.shape
    words = np.ascontiguousarray(words).reshape(g, 128, n, -1)
    if fmt in ("e4m3", "e5m2"):
        vals = words.view(ml_dtypes.float8_e4m3fn if fmt == "e4m3" else ml_dtypes.float8_e5m2).astype(np.float64)
    else:
        nib = np.empty((g, 128, n, 4), np.uint8)
        nib[..., 0::2] = words & 0xF
        nib[..., 1::2] = words >> 4
        vals = E2M1[nib]
    vals = vals * np.repeat(np.exp2(scales.astype(np.float64) - 127.0), 8, axis=1)[..., None]
    return vals.transpose(0, 1, 3, 2).reshape(g * 512, n)


K, T, J, R, V, O, N, S, E = 512, 1024, 256, 512, 1024, 128, 256, 1024, 1024


def setup_inputs():
    n = np.random.standard_normal
    idx = np.random.permutation(V)[:R]
    idx2 = np.random.permutation(T)[:J]
    idx3 = np.stack([np.random.permutation(J)[:O] for _ in range(8)])
    idx4 = np.stack([np.random.permutation(J)[:O] for _ in range(8)])
    idx5 = np.random.permutation(S)[:N]
    idx6 = np.random.permutation(E)[:O]
    fk = mx_kscale(K)
    fr = mx_kscale(R)
    tr = np.ones(V)
    tr[idx] = fr
    xtp = pack_weight(n((K, T)) / fk[:, None], "e2m1")
    wtp = pack_weight(n((K, V)) * 1 / np.sqrt(K) * fk[:, None] * tr, "e4m3")
    w2p = pack_weight(n((K, R)) * 1 / np.sqrt(K) * fk[:, None], "e5m2")
    vsp = pack_weight(n((R, S)) * 1 / np.sqrt(R) / fr[:, None], "e2m1")
    return {
        "xt_words": xtp[0],
        "xt_scales": xtp[1],
        "wt_words": wtp[0],
        "wt_scales": wtp[1],
        "w2_words": w2p[0],
        "w2_scales": w2p[1],
        "vs_words": vsp[0],
        "vs_scales": vsp[1],
        "offs": striped(idx),
        "offs2": striped(idx2),
        "offs3": striped8(idx3),
        "offs4": striped8(idx4),
        "offs5": striped(idx5),
        "offs6": striped(idx6),
    }


def reference(xt_words, xt_scales, wt_words, wt_scales, w2_words, w2_scales, vs_words, vs_scales, offs, offs2, offs3, offs4, offs5, offs6):
    idx = unstriped(offs)
    idx2 = unstriped(offs2)
    idx3 = unstriped8(offs3)
    idx4 = unstriped8(offs4)
    idx5 = unstriped(offs5)
    idx6 = unstriped(offs6)
    xtu = unpack_weight(xt_words, xt_scales, "e2m1")
    wtu = unpack_weight(wt_words, wt_scales, "e4m3")
    w2u = unpack_weight(w2_words, w2_scales, "e5m2")
    vsu = unpack_weight(vs_words, vs_scales, "e2m1")
    wtidxg = wtu[:, idx]
    xtidx2g = xtu[:, idx2]
    a = wtidxg.T @ xtidx2g
    b = w2u.T @ xtidx2g
    lb = b[:, 0:1]
    la = a[:, 0:1]
    hid = np.abs(pick8(a, idx3, 64) * lb - pick8(b, idx4, 64) * la)
    vsidx5g = vsu[:, idx5]
    hidq = mxq(hid, 0, "e5m2")
    p = vsidx5g.T @ hidq
    y = np.zeros((N, E))
    y[:, idx6] = p
    return y

@@ -1,0 +1,149 @@
+from contextlib import ExitStack
+
+import concourse.mybir as mybir
+
+F32 = mybir.dt.float32
+BF16 = mybir.dt.bfloat16
+I32 = mybir.dt.int32
+U32 = mybir.dt.uint32
+U16 = mybir.dt.uint16
+U8 = mybir.dt.uint8
+E4M3X4 = mybir.dt.float8_e4m3fn_x4
+E5M2X4 = mybir.dt.float8_e5m2_x4
+E2M1X4 = mybir.dt.float4_e2m1fn_x4
+ACT = mybir.ActivationFunctionType
+ALU = mybir.AluOpType
+
+K, T, J, R, V, O, N, S, E = 512, 1024, 256, 512, 1024, 128, 256, 1024, 1024
+P = 128
+PACK = 4
+FLOPS = 2 * K * R * J * 2 + 2 * R * N * O
+
+
+def tile_list_groupleads_storeleads_store_scattered_kernel(
+    tc, xt_words, xt_scales, wt_words, wt_scales, w2_words, w2_scales, vs_words, vs_scales,
+    offs, offs2, offs3, offs4, offs5, offs6, out,
+):
+    nc = tc.nc
+    with ExitStack() as ctx:
+        sb = ctx.enter_context(tc.tile_pool(name="sb", bufs=1))
+        ps = ctx.enter_context(tc.psum_pool(name="ps", bufs=1))
+
+        def tile(name, shape, dtype):
+            return sb.tile(shape, dtype, name=name, align_bytes=64)
+
+        def load_list(name, src):
+            t = tile(name, list(src.shape), U16)
+            nc.sync.dma_start(t[:], src)
+            return t
+
+        def zeroed_plane(name, cols):
+            t = tile(name, [P, cols], U8)
+            nc.vector.memset(t[:].bitcast(I32), 0)
+            return t
+
+        def load_plane(t, src):
+            for q in range(4):
+                nc.sync.dma_start(t[32 * q : 32 * q + 4, :].bitcast(I32), src[0, 4 * q : 4 * q + 4, :].bitcast(I32))
+
+        def load_words(name, cols, dtype, src):
+            t = tile(name, [P, cols], dtype)
+            nc.sync.dma_start(t[:].bitcast(I32), src.bitcast(I32))
+            return t
+
+        xs = zeroed_plane("xs", T)
+        ws = zeroed_plane("ws", V)
+        w2s = zeroed_plane("w2s", R)
+        vs = zeroed_plane("vs", S)
+        pages = [tile(f"page{h}", [P, E], F32) for h in range(2)]
+        for page in pages:
+            nc.vector.memset(page[:], 0.0)
+
+        l2 = load_list("l2", offs2)
+        load_plane(xs, xt_scales)
+        xw = load_words("xw", T, U16, xt_words[0])
+        l1 = load_list("l1", offs)
+        ww = load_words("ww", V, U32, wt_words[0].rearrange("p n t -> p (n t)"))
+        load_plane(ws, wt_scales)
+        w2w = load_words("w2w", R, U32, w2_words[0].rearrange("p n t -> p (n t)"))
+        load_plane(w2s, w2_scales)
+        l3 = load_list("l3", offs3)
+        l4 = load_list("l4", offs4)
+        vw = load_words("vw", S, U16, vs_words[0])
+        load_plane(vs, vs_scales)
+        l5 = load_list("l5", offs5)
+        l6 = load_list("l6", offs6)
+
+        xsg = tile("xsg", [P, J], U8)
+        xwg = tile("xwg", [P, J], U16)
+        nc.vector.tensor_copy(xsg[:], xs[:].indirect(l2[:]))
+        nc.vector.tensor_copy(xwg[:], xw[:].indirect(l2[:]))
+
+        wwg = tile("wwg", [P, PACK, P], U32)
+        wsg = tile("wsg", [P, PACK, P], U8)
+        nc.vector.tensor_copy(wwg[:].rearrange("p t q -> p q t"), ww[:].indirect(l1[:]))
+
+        w2wd = tile("w2wd", [P, PACK, P], U32)
+        w2sd = tile("w2sd", [P, PACK, P], U8)
+        nc.scalar.copy(w2wd[:].rearrange("p t q -> p q t"), w2w[:].rearrange("p (q t) -> p q t", t=PACK))
+        nc.vector.tensor_copy(w2sd[:], w2s[:].rearrange("p (q t) -> p t q", t=PACK))
+
+        nc.vector.tensor_copy(wsg[:].rearrange("p t q -> p q t"), ws[:].indirect(l1[:]))
+
+        b_banks = [ps.tile([P, 2, J], F32, name=f"b_bank{i}") for i in range(2)]
+        b_rows = [tile(f"b_rows{t}", [P, J], F32) for t in range(PACK)]
+        for t in range(PACK):
+            nc.tensor.matmul_mx(
+                out=b_banks[t // 2][:, t % 2, :],
+                lhsT=w2wd[:, t, :].bitcast(E5M2X4), lhsT_scale=w2sd[:, t, :],
+                rhs=xwg[:].bitcast(E2M1X4), rhs_scale=xsg[:], start=True, stop=True,
+            )
+        for t in range(PACK):
+            nc.scalar.activation(b_rows[t][:], b_banks[t // 2][:, t % 2, :], ACT.Copy)
+
+        a_banks = [ps.tile([P, J], F32, name=f"a_bank{t}") for t in range(PACK)]
+        a_rows = [tile(f"a_rows{t}", [P, J], F32) for t in range(PACK)]
+        for t in range(PACK):
+            nc.tensor.matmul_mx(
+                out=a_banks[t][:],
+                lhsT=wwg[:, t, :].bitcast(E4M3X4), lhsT_scale=wsg[:, t, :],
+                rhs=xwg[:].bitcast(E2M1X4), rhs_scale=xsg[:], start=True, stop=True,
+            )
+        for t in range(PACK):
+            nc.vector.tensor_copy(a_rows[t][:], a_banks[t][:])
+
+        vwg = tile("vwg", [P, N], U16)
+        vsg = tile("vsg", [P, N], U8)
+        nc.vector.tensor_copy(vwg[:], vw[:].indirect(l5[:]))
+        nc.vector.tensor_copy(vsg[:], vs[:].indirect(l5[:]))
+
+        a_pick = tile("a_pick", [P, PACK, O], F32)
+        b_pick = tile("b_pick", [P, PACK, O], F32)
+        diff = tile("diff", [P, PACK, O], F32)
+        for t in range(PACK):
+            nc.scalar.activation(a_pick[:, t, :], a_rows[t][:].indirect(l3[:]), ACT.Copy, scale=b_rows[t][:, 0:1])
+            nc.scalar.activation(b_pick[:, t, :], b_rows[t][:].indirect(l4[:]), ACT.Copy, scale=a_rows[t][:, 0:1])
+            nc.vector.tensor_tensor(diff[:, t, :], a_pick[:, t, :], b_pick[:, t, :], ALU.subtract)
+
+        hid = tile("hid", [P, O, PACK], BF16)
+        nc.scalar.activation(hid[:], diff[:].rearrange("p t o -> p o t"), ACT.Abs)
+        hw = tile("hw", [P, O], U32)
+        hs = tile("hs", [P, O], U8)
+        nc.vector.quantize_mx(out=hw[:].bitcast(E5M2X4), scales=hs[:], in_=hid[:].rearrange("p o t -> p (o t)"))
+
+        for h in range(2):
+            cols = slice(P * h, P * (h + 1))
+            bank = ps.tile([P, O], F32, name=f"p_bank{h}")
+            nc.tensor.matmul_mx(
+                out=bank[:], lhsT=vwg[:, cols].bitcast(E2M1X4), lhsT_scale=vsg[:, cols],
+                rhs=hw[:].bitcast(E5M2X4), rhs_scale=hs[:], start=True, stop=True,
+            )
+            rows = tile(f"p_rows{h}", [P, O], F32)
+            if h == 0:
+                nc.vector.tensor_copy(rows[:], bank[:])
+                nc.vector.tensor_copy(pages[h][:].indirect(l6[:]), rows[:])
+                nc.sync.dma_start(out[cols, :], pages[h][:])
+            else:
+                nc.scalar.copy(rows[:], bank[:])
+                nc.scalar.activation(pages[h][:].indirect(l6[:]), rows[:], ACT.Copy)
+                nc.scalar.dma_start(out[cols, :], pages[h][:])

@@ -29,65 +29,66 @@ def tile_list_groupleads_storeleads_store_scattered_kernel(
         sb = ctx.enter_context(tc.tile_pool(name="sb", bufs=1))
         ps = ctx.enter_context(tc.psum_pool(name="ps", bufs=1))
 
-        def tile(name, shape, dtype):
-            return sb.tile(shape, dtype, name=name, align_bytes=64)
+        def tile(name, shape, dtype, tag=None):
+            return sb.tile(shape, dtype, name=name, tag=tag or name, align_bytes=64)
 
         def load_list(name, src):
             t = tile(name, list(src.shape), U16)
             nc.sync.dma_start(t[:], src)
             return t
 
-        def zeroed_plane(name, cols):
+        def zeroed_plane(name, cols, eng):
             t = tile(name, [P, cols], U8)
-            nc.vector.memset(t[:].bitcast(I32), 0)
+            eng.memset(t[:].bitcast(I32), 0)
             return t
 
-        def load_plane(t, src):
-            for q in range(4):
-                nc.sync.dma_start(t[32 * q : 32 * q + 4, :].bitcast(I32), src[0, 4 * q : 4 * q + 4, :].bitcast(I32))
+        def load_plane(t, src, quads=range(4), eng=nc.sync):
+            for q in quads:
+                eng.dma_start(t[32 * q : 32 * q + 4, :].bitcast(I32), src[0, 4 * q : 4 * q + 4, :].bitcast(I32))
 
         def load_words(name, cols, dtype, src):
             t = tile(name, [P, cols], dtype)
             nc.sync.dma_start(t[:].bitcast(I32), src.bitcast(I32))
             return t
 
-        xs = zeroed_plane("xs", T)
-        ws = zeroed_plane("ws", V)
-        w2s = zeroed_plane("w2s", R)
-        vs = zeroed_plane("vs", S)
+        xs = zeroed_plane("xs", T, nc.vector)
+        ws = zeroed_plane("ws", V, nc.gpsimd)
+        w2s = zeroed_plane("w2s", R, nc.vector)
+        vs = zeroed_plane("vs", S, nc.vector)
         pages = [tile(f"page{h}", [P, E], F32) for h in range(2)]
         for page in pages:
             nc.vector.memset(page[:], 0.0)
 
         l2 = load_list("l2", offs2)
-        load_plane(xs, xt_scales)
         xw = load_words("xw", T, U16, xt_words[0])
+        load_plane(xs, xt_scales)
         l1 = load_list("l1", offs)
         ww = load_words("ww", V, U32, wt_words[0].rearrange("p n t -> p (n t)"))
-        load_plane(ws, wt_scales)
+        load_plane(ws, wt_scales, range(2), nc.gpsimd)
         w2w = load_words("w2w", R, U32, w2_words[0].rearrange("p n t -> p (n t)"))
         load_plane(w2s, w2_scales)
+        load_plane(ws, wt_scales, range(2, 4))
         l3 = load_list("l3", offs3)
         l4 = load_list("l4", offs4)
-        vw = load_words("vw", S, U16, vs_words[0])
-        load_plane(vs, vs_scales)
         l5 = load_list("l5", offs5)
+        load_plane(vs, vs_scales)
+        vw = load_words("vw", S, U16, vs_words[0])
         l6 = load_list("l6", offs6)
 
         xsg = tile("xsg", [P, J], U8)
         xwg = tile("xwg", [P, J], U16)
-        nc.vector.tensor_copy(xsg[:], xs[:].indirect(l2[:]))
         nc.vector.tensor_copy(xwg[:], xw[:].indirect(l2[:]))
+        nc.vector.tensor_copy(xsg[:], xs[:].indirect(l2[:]))
 
         wwg = tile("wwg", [P, PACK, P], U32)
         wsg = tile("wsg", [P, PACK, P], U8)
-        nc.vector.tensor_copy(wwg[:].rearrange("p t q -> p q t"), ww[:].indirect(l1[:]))
 
         w2wd = tile("w2wd", [P, PACK, P], U32)
         w2sd = tile("w2sd", [P, PACK, P], U8)
         nc.scalar.copy(w2wd[:].rearrange("p t q -> p q t"), w2w[:].rearrange("p (q t) -> p q t", t=PACK))
         nc.vector.tensor_copy(w2sd[:], w2s[:].rearrange("p (q t) -> p t q", t=PACK))
 
+        nc.vector.tensor_copy(wwg[:].rearrange("p t q -> p q t"), ww[:].indirect(l1[:]))
         nc.vector.tensor_copy(wsg[:].rearrange("p t q -> p q t"), ws[:].indirect(l1[:]))
 
         b_banks = [ps.tile([P, 2, J], F32, name=f"b_bank{i}") for i in range(2)]
@@ -102,31 +103,34 @@ def tile_list_groupleads_storeleads_store_scattered_kernel(
             nc.scalar.activation(b_rows[t][:], b_banks[t // 2][:, t % 2, :], ACT.Copy)
 
         a_banks = [ps.tile([P, J], F32, name=f"a_bank{t}") for t in range(PACK)]
-        a_rows = [tile(f"a_rows{t}", [P, J], F32) for t in range(PACK)]
+        a_tags = [None, None, None, "vs"]
+        a_rows = [tile(f"a_rows{t}", [P, J], F32, a_tags[t]) for t in range(PACK)]
         for t in range(PACK):
             nc.tensor.matmul_mx(
                 out=a_banks[t][:],
                 lhsT=wwg[:, t, :].bitcast(E4M3X4), lhsT_scale=wsg[:, t, :],
                 rhs=xwg[:].bitcast(E2M1X4), rhs_scale=xsg[:], start=True, stop=True,
             )
+        vwg = tile("vwg", [P, N], U16)
+        vsg = tile("vsg", [P, N], U8)
+        nc.vector.tensor_copy(vsg[:], vs[:].indirect(l5[:]))
+        nc.vector.tensor_copy(vwg[:], vw[:].indirect(l5[:]))
         for t in range(PACK):
             nc.vector.tensor_copy(a_rows[t][:], a_banks[t][:])
 
-        vwg = tile("vwg", [P, N], U16)
-        vsg = tile("vsg", [P, N], U8)
-        nc.vector.tensor_copy(vwg[:], vw[:].indirect(l5[:]))
-        nc.vector.tensor_copy(vsg[:], vs[:].indirect(l5[:]))
-
         a_pick = tile("a_pick", [P, PACK, O], F32)
         b_pick = tile("b_pick", [P, PACK, O], F32)
-        diff = tile("diff", [P, PACK, O], F32)
+        diff = tile("diff", [P, PACK, O], F32, "vw")
         for t in range(PACK):
             nc.scalar.activation(a_pick[:, t, :], a_rows[t][:].indirect(l3[:]), ACT.Copy, scale=b_rows[t][:, 0:1])
             nc.scalar.activation(b_pick[:, t, :], b_rows[t][:].indirect(l4[:]), ACT.Copy, scale=a_rows[t][:, 0:1])
             nc.vector.tensor_tensor(diff[:, t, :], a_pick[:, t, :], b_pick[:, t, :], ALU.subtract)
 
         hid = tile("hid", [P, O, PACK], BF16)
-        nc.scalar.activation(hid[:], diff[:].rearrange("p t o -> p o t"), ACT.Abs)
+        by_place = diff[:].rearrange("p t o -> p o t")
+        half = 96
+        nc.scalar.activation(hid[:, :half, :], by_place[:, :half, :], ACT.Abs)
+        nc.vector.scalar_tensor_tensor(hid[:, half:, :], by_place[:, half:, :], -1.0, by_place[:, half:, :], ALU.mult, ALU.max)
         hw = tile("hw", [P, O], U32)
         hs = tile("hs", [P, O], U8)
         nc.vector.quantize_mx(out=hw[:].bitcast(E5M2X4), scales=hs[:], in_=hid[:].rearrange("p o t -> p (o t)"))
@@ -140,10 +144,10 @@ def tile_list_groupleads_storeleads_store_scattered_kernel(
             )
             rows = tile(f"p_rows{h}", [P, O], F32)
             if h == 0:
-                nc.vector.tensor_copy(rows[:], bank[:])
+                nc.scalar.copy(rows[:], bank[:])
                 nc.vector.tensor_copy(pages[h][:].indirect(l6[:]), rows[:])
                 nc.sync.dma_start(out[cols, :], pages[h][:])
             else:
-                nc.scalar.copy(rows[:], bank[:])
+                nc.vector.tensor_copy(rows[:], bank[:])
                 nc.scalar.activation(pages[h][:].indirect(l6[:]), rows[:], ACT.Copy)
                 nc.scalar.dma_start(out[cols, :], pages[h][:])

@@ -55,21 +55,20 @@ def tile_list_groupleads_storeleads_store_scattered_kernel(
         ws = zeroed_plane("ws", V, nc.gpsimd)
         w2s = zeroed_plane("w2s", R, nc.vector)
         vs = zeroed_plane("vs", S, nc.vector)
-        pages = [tile(f"page{h}", [P, E], F32) for h in range(2)]
-        for page in pages:
-            nc.vector.memset(page[:], 0.0)
+        page0 = tile("page0", [P, E], F32)
+        nc.vector.memset(page0[:], 0.0)
 
         l2 = load_list("l2", offs2)
         xw = load_words("xw", T, U16, xt_words[0])
-        load_plane(xs, xt_scales)
         l1 = load_list("l1", offs)
+        load_plane(xs, xt_scales)
         ww = load_words("ww", V, U32, wt_words[0].rearrange("p n t -> p (n t)"))
         load_plane(ws, wt_scales, range(2), nc.gpsimd)
         w2w = load_words("w2w", R, U32, w2_words[0].rearrange("p n t -> p (n t)"))
         load_plane(w2s, w2_scales)
         load_plane(ws, wt_scales, range(2, 4))
-        l3 = load_list("l3", offs3)
         l4 = load_list("l4", offs4)
+        l3 = load_list("l3", offs3)
         l5 = load_list("l5", offs5)
         load_plane(vs, vs_scales)
         vw = load_words("vw", S, U16, vs_words[0])
@@ -86,45 +85,50 @@ def tile_list_groupleads_storeleads_store_scattered_kernel(
         w2wd = tile("w2wd", [P, PACK, P], U32)
         w2sd = tile("w2sd", [P, PACK, P], U8)
         nc.scalar.copy(w2wd[:].rearrange("p t q -> p q t"), w2w[:].rearrange("p (q t) -> p q t", t=PACK))
-        nc.vector.tensor_copy(w2sd[:], w2s[:].rearrange("p (q t) -> p t q", t=PACK))
+        nc.gpsimd.tensor_copy(w2sd[:], w2s[:].rearrange("p (q t) -> p t q", t=PACK))
+
+        page1 = tile("page1", [P, E], F32, "w2s")
+        nc.gpsimd.memset(page1[:], 0.0)
+        pages = [page0, page1]
 
         nc.vector.tensor_copy(wwg[:].rearrange("p t q -> p q t"), ww[:].indirect(l1[:]))
         nc.vector.tensor_copy(wsg[:].rearrange("p t q -> p q t"), ws[:].indirect(l1[:]))
 
-        b_banks = [ps.tile([P, 2, J], F32, name=f"b_bank{i}") for i in range(2)]
-        b_rows = [tile(f"b_rows{t}", [P, J], F32) for t in range(PACK)]
-        for t in range(PACK):
+        def product(name, words, scales, tag):
+            bank = ps.tile([P, J], F32, name=name, tag=tag)
             nc.tensor.matmul_mx(
-                out=b_banks[t // 2][:, t % 2, :],
-                lhsT=w2wd[:, t, :].bitcast(E5M2X4), lhsT_scale=w2sd[:, t, :],
+                out=bank[:], lhsT=words, lhsT_scale=scales,
                 rhs=xwg[:].bitcast(E2M1X4), rhs_scale=xsg[:], start=True, stop=True,
             )
-        for t in range(PACK):
-            nc.scalar.activation(b_rows[t][:], b_banks[t // 2][:, t % 2, :], ACT.Copy)
+            return bank
 
-        a_banks = [ps.tile([P, J], F32, name=f"a_bank{t}") for t in range(PACK)]
+        b_rows = [tile(f"b_rows{t}", [P, J], F32) for t in range(PACK)]
         a_tags = [None, None, None, "vs"]
         a_rows = [tile(f"a_rows{t}", [P, J], F32, a_tags[t]) for t in range(PACK)]
-        for t in range(PACK):
-            nc.tensor.matmul_mx(
-                out=a_banks[t][:],
-                lhsT=wwg[:, t, :].bitcast(E4M3X4), lhsT_scale=wsg[:, t, :],
-                rhs=xwg[:].bitcast(E2M1X4), rhs_scale=xsg[:], start=True, stop=True,
-            )
         vwg = tile("vwg", [P, N], U16)
         vsg = tile("vsg", [P, N], U8)
         nc.vector.tensor_copy(vsg[:], vs[:].indirect(l5[:]))
         nc.vector.tensor_copy(vwg[:], vw[:].indirect(l5[:]))
+
         for t in range(PACK):
-            nc.vector.tensor_copy(a_rows[t][:], a_banks[t][:])
+            bank = product(f"b_bank{t}", w2wd[:, t, :].bitcast(E5M2X4), w2sd[:, t, :], f"early{t}")
+            nc.scalar.copy(b_rows[t][:], bank[:])
+        for t in range(PACK):
+            bank = product(f"a_bank{t}", wwg[:, t, :].bitcast(E4M3X4), wsg[:, t, :], f"late{t}")
+            if t == 0:
+                nc.vector.tensor_copy(a_rows[t][:, :8], bank[:, :8])
+                nc.vector.tensor_copy(a_rows[t][:, 8:], bank[:, 8:])
+            else:
+                nc.vector.tensor_copy(a_rows[t][:], bank[:])
 
         a_pick = tile("a_pick", [P, PACK, O], F32)
         b_pick = tile("b_pick", [P, PACK, O], F32)
         diff = tile("diff", [P, PACK, O], F32, "vw")
         for t in range(PACK):
-            nc.scalar.activation(a_pick[:, t, :], a_rows[t][:].indirect(l3[:]), ACT.Copy, scale=b_rows[t][:, 0:1])
             nc.scalar.activation(b_pick[:, t, :], b_rows[t][:].indirect(l4[:]), ACT.Copy, scale=a_rows[t][:, 0:1])
-            nc.vector.tensor_tensor(diff[:, t, :], a_pick[:, t, :], b_pick[:, t, :], ALU.subtract)
+            nc.scalar.activation(a_pick[:, t, :], a_rows[t][:].indirect(l3[:]), ACT.Copy, scale=b_rows[t][:, 0:1])
+        for part in (slice(0, PACK - 1), slice(PACK - 1, PACK)):
+            nc.vector.tensor_tensor(diff[:, part, :], a_pick[:, part, :], b_pick[:, part, :], ALU.subtract)
 
         hid = tile("hid", [P, O, PACK], BF16)
         by_place = diff[:].rearrange("p t o -> p o t")
@@ -137,7 +141,7 @@ def tile_list_groupleads_storeleads_store_scattered_kernel(
 
         for h in range(2):
             cols = slice(P * h, P * (h + 1))
-            bank = ps.tile([P, O], F32, name=f"p_bank{h}")
+            bank = ps.tile([P, O], F32, name=f"p_bank{h}", tag=f"early{h}")
             nc.tensor.matmul_mx(
                 out=bank[:], lhsT=vwg[:, cols].bitcast(E2M1X4), lhsT_scale=vsg[:, cols],
                 rhs=hw[:].bitcast(E5M2X4), rhs_scale=hs[:], start=True, stop=True,

from contextlib import ExitStack

import concourse.mybir as mybir

F32 = mybir.dt.float32
BF16 = mybir.dt.bfloat16
I32 = mybir.dt.int32
U32 = mybir.dt.uint32
U16 = mybir.dt.uint16
U8 = mybir.dt.uint8
E4M3X4 = mybir.dt.float8_e4m3fn_x4
E5M2X4 = mybir.dt.float8_e5m2_x4
E2M1X4 = mybir.dt.float4_e2m1fn_x4
ACT = mybir.ActivationFunctionType
ALU = mybir.AluOpType

K, T, J, R, V, O, N, S, E = 512, 1024, 256, 512, 1024, 128, 256, 1024, 1024
P = 128
PACK = 4
FLOPS = 2 * K * R * J * 2 + 2 * R * N * O


def tile_list_groupleads_storeleads_store_scattered_kernel(
    tc, xt_words, xt_scales, wt_words, wt_scales, w2_words, w2_scales, vs_words, vs_scales,
    offs, offs2, offs3, offs4, offs5, offs6, out,
):
    nc = tc.nc
    with ExitStack() as ctx:
        sb = ctx.enter_context(tc.tile_pool(name="sb", bufs=1))
        ps = ctx.enter_context(tc.psum_pool(name="ps", bufs=1))

        def tile(name, shape, dtype, tag=None):
            return sb.tile(shape, dtype, name=name, tag=tag or name, align_bytes=64)

        def load_list(name, src):
            t = tile(name, list(src.shape), U16)
            nc.sync.dma_start(t[:], src)
            return t

        def zeroed_plane(name, cols, eng):
            t = tile(name, [P, cols], U8)
            eng.memset(t[:].bitcast(I32), 0)
            return t

        def load_plane(t, src, quads=range(4), eng=nc.sync):
            for q in quads:
                eng.dma_start(t[32 * q : 32 * q + 4, :].bitcast(I32), src[0, 4 * q : 4 * q + 4, :].bitcast(I32))

        def load_words(name, cols, dtype, src):
            t = tile(name, [P, cols], dtype)
            nc.sync.dma_start(t[:].bitcast(I32), src.bitcast(I32))
            return t

        xs = zeroed_plane("xs", T, nc.vector)
        ws = zeroed_plane("ws", V, nc.gpsimd)
        w2s = zeroed_plane("w2s", R, nc.vector)
        vs = zeroed_plane("vs", S, nc.vector)
        page0 = tile("page0", [P, E], F32)
        nc.vector.memset(page0[:], 0.0)

        l2 = load_list("l2", offs2)
        xw = load_words("xw", T, U16, xt_words[0])
        l1 = load_list("l1", offs)
        load_plane(xs, xt_scales)
        ww = load_words("ww", V, U32, wt_words[0].rearrange("p n t -> p (n t)"))
        load_plane(ws, wt_scales, range(2), nc.gpsimd)
        w2w = load_words("w2w", R, U32, w2_words[0].rearrange("p n t -> p (n t)"))
        load_plane(w2s, w2_scales)
        load_plane(ws, wt_scales, range(2, 4))
        l4 = load_list("l4", offs4)
        l3 = load_list("l3", offs3)
        l5 = load_list("l5", offs5)
        load_plane(vs, vs_scales)
        vw = load_words("vw", S, U16, vs_words[0])
        l6 = load_list("l6", offs6)

        xsg = tile("xsg", [P, J], U8)
        xwg = tile("xwg", [P, J], U16)
        nc.vector.tensor_copy(xwg[:], xw[:].indirect(l2[:]))
        nc.vector.tensor_copy(xsg[:], xs[:].indirect(l2[:]))

        wwg = tile("wwg", [P, PACK, P], U32)
        wsg = tile("wsg", [P, PACK, P], U8)

        w2wd = tile("w2wd", [P, PACK, P], U32)
        w2sd = tile("w2sd", [P, PACK, P], U8)
        nc.scalar.copy(w2wd[:].rearrange("p t q -> p q t"), w2w[:].rearrange("p (q t) -> p q t", t=PACK))
        nc.gpsimd.tensor_copy(w2sd[:], w2s[:].rearrange("p (q t) -> p t q", t=PACK))

        page1 = tile("page1", [P, E], F32, "w2s")
        nc.gpsimd.memset(page1[:], 0.0)
        pages = [page0, page1]

        nc.vector.tensor_copy(wwg[:].rearrange("p t q -> p q t"), ww[:].indirect(l1[:]))
        nc.vector.tensor_copy(wsg[:].rearrange("p t q -> p q t"), ws[:].indirect(l1[:]))

        def product(name, words, scales, tag):
            bank = ps.tile([P, J], F32, name=name, tag=tag)
            nc.tensor.matmul_mx(
                out=bank[:], lhsT=words, lhsT_scale=scales,
                rhs=xwg[:].bitcast(E2M1X4), rhs_scale=xsg[:], start=True, stop=True,
            )
            return bank

        b_rows = [tile(f"b_rows{t}", [P, J], F32) for t in range(PACK)]
        a_tags = [None, None, None, "vs"]
        a_rows = [tile(f"a_rows{t}", [P, J], F32, a_tags[t]) for t in range(PACK)]
        vwg = tile("vwg", [P, N], U16)
        vsg = tile("vsg", [P, N], U8)
        nc.vector.tensor_copy(vsg[:], vs[:].indirect(l5[:]))
        nc.vector.tensor_copy(vwg[:], vw[:].indirect(l5[:]))

        for t in range(PACK):
            bank = product(f"b_bank{t}", w2wd[:, t, :].bitcast(E5M2X4), w2sd[:, t, :], f"early{t}")
            nc.scalar.copy(b_rows[t][:], bank[:])
        for t in range(PACK):
            bank = product(f"a_bank{t}", wwg[:, t, :].bitcast(E4M3X4), wsg[:, t, :], f"late{t}")
            if t == 0:
                nc.vector.tensor_copy(a_rows[t][:, :8], bank[:, :8])
                nc.vector.tensor_copy(a_rows[t][:, 8:], bank[:, 8:])
            else:
                nc.vector.tensor_copy(a_rows[t][:], bank[:])

        a_pick = tile("a_pick", [P, PACK, O], F32)
        b_pick = tile("b_pick", [P, PACK, O], F32)
        diff = tile("diff", [P, PACK, O], F32, "vw")
        for t in range(PACK):
            nc.scalar.activation(b_pick[:, t, :], b_rows[t][:].indirect(l4[:]), ACT.Copy, scale=a_rows[t][:, 0:1])
            nc.scalar.activation(a_pick[:, t, :], a_rows[t][:].indirect(l3[:]), ACT.Copy, scale=b_rows[t][:, 0:1])
        for part in (slice(0, PACK - 1), slice(PACK - 1, PACK)):
            nc.vector.tensor_tensor(diff[:, part, :], a_pick[:, part, :], b_pick[:, part, :], ALU.subtract)

        hid = tile("hid", [P, O, PACK], BF16)
        by_place = diff[:].rearrange("p t o -> p o t")
        half = 96
        nc.scalar.activation(hid[:, :half, :], by_place[:, :half, :], ACT.Abs)
        nc.vector.scalar_tensor_tensor(hid[:, half:, :], by_place[:, half:, :], -1.0, by_place[:, half:, :], ALU.mult, ALU.max)
        hw = tile("hw", [P, O], U32)
        hs = tile("hs", [P, O], U8)
        nc.vector.quantize_mx(out=hw[:].bitcast(E5M2X4), scales=hs[:], in_=hid[:].rearrange("p o t -> p (o t)"))

        for h in range(2):
            cols = slice(P * h, P * (h + 1))
            bank = ps.tile([P, O], F32, name=f"p_bank{h}", tag=f"early{h}")
            nc.tensor.matmul_mx(
                out=bank[:], lhsT=vwg[:, cols].bitcast(E2M1X4), lhsT_scale=vsg[:, cols],
                rhs=hw[:].bitcast(E5M2X4), rhs_scale=hs[:], start=True, stop=True,
            )
            rows = tile(f"p_rows{h}", [P, O], F32)
            if h == 0:
                nc.scalar.copy(rows[:], bank[:])
                nc.vector.tensor_copy(pages[h][:].indirect(l6[:]), rows[:])
                nc.sync.dma_start(out[cols, :], pages[h][:])
            else:
                nc.vector.tensor_copy(rows[:], bank[:])
                nc.scalar.activation(pages[h][:].indirect(l6[:]), rows[:], ACT.Copy)
                nc.scalar.dma_start(out[cols, :], pages[h][:])
